import numpy as np
import ml_dtypes


def mxq(x, axis, fmt="e4m3"):
    dtype, down = {"e4m3": (ml_dtypes.float8_e4m3fn, 7), "e5m2": (ml_dtypes.float8_e5m2, 14)}[fmt]
    v = np.moveaxis(np.asarray(x, np.float32).astype(ml_dtypes.bfloat16).astype(np.float64), axis, -1)
    blocks = v.reshape(v.shape[:-1] + (-1, 32))
    amax = np.abs(blocks).max(-1, keepdims=True)
    byte = np.maximum(np.where(amax > 0, np.frexp(amax)[1] - 1 + 127, 0) - down, 1)
    scale = np.exp2(byte - 127.0)
    codes = (blocks / scale).astype(np.float32).astype(dtype).astype(np.float64)
    return np.moveaxis((codes * scale).reshape(v.shape), -1, axis)


WIDE = False


def mx_kscale(k):
    if not WIDE:
        return np.ones(k)
    levels = np.array([30, -30])
    if k % 512:
        return np.exp2(np.random.permutation(np.resize(levels, k // 32))).repeat(32)
    a = np.empty((k // 512, 16))
    for p in range(k // 512):
        a[p, :8] = np.random.permutation(np.resize(levels, 8))
        for g in range(8):
            far = levels[np.abs(levels - a[p, g]) >= 10]
            a[p, g + 8] = far[np.random.randint(len(far))]
    return np.exp2(a.ravel()).repeat(32)


def f64(x):
    return np.asarray(x).astype(np.float64)


def striped(idx):
    return np.tile(np.asarray(idx).reshape(-1, 16).T, (8, 1)).astype(np.uint16)


def unstriped(offs):
    return offs[:16].T.reshape(-1).astype(np.int64)


E2M1 = np.array([0.0, 0.5, 1.0, 1.5, 2.0, 3.0, 4.0, 6.0, -0.0, -0.5, -1.0, -1.5, -2.0, -3.0, -4.0, -6.0])


def pack_weight(w, fmt):
    k, n = w.shape
    w = f64(np.asarray(w, np.float32).astype(ml_dtypes.bfloat16)).reshape(k // 32, 32, n)
    amax = np.abs(w).max(1)
    if fmt == "e4m3":
        byte = np.frexp(amax)[1] - 1 + 127 - 7
    else:
        mant, ex = np.frexp(amax / 6.0)
        byte = np.where(mant > 0.5, ex, ex - 1) + 127
    byte = np.clip(np.where(amax > 0, byte, 1), 1, 254)
    scaled = (w * np.exp2(127.0 - byte)[:, None, :]).reshape(k, n).astype(np.float32)
    by_word = np.ascontiguousarray(scaled.reshape(k // 512, 128, 4, n).transpose(0, 1, 3, 2))
    if fmt == "e4m3":
        words = by_word.astype(ml_dtypes.float8_e4m3fn).view(np.uint8)
    else:
        c = by_word.astype(ml_dtypes.float4_e2m1fn).view(np.uint8) & 0xF
        words = (c[..., 0::2] | (c[..., 1::2] << 4)).reshape(k // 512, 128, 2 * n)
    return np.ascontiguousarray(words), np.ascontiguousarray(byte.astype(np.uint8).reshape(k // 512, 16, n))


def unpack_weight(words, scales, fmt):
    g, _, n = scales.shape
    words = np.ascontiguousarray(words).reshape(g, 128, n, -1)
    if fmt == "e4m3":
        vals = words.view(ml_dtypes.float8_e4m3fn).astype(np.float64)
    else:
        nib = np.empty((g, 128, n, 4), np.uint8)
        nib[..., 0::2] = words & 0xF
        nib[..., 1::2] = words >> 4
        vals = E2M1[nib]
    vals = vals * np.repeat(np.exp2(scales.astype(np.float64) - 127.0), 8, axis=1)[..., None]
    return vals.transpose(0, 1, 3, 2).reshape(g * 512, n)


def sigmoid(v):
    return 1.0 / (1.0 + np.exp(-v))


def sgn(shape):
    return np.random.uniform(0.5, 2.0, shape) * np.where(np.random.standard_normal(shape) < 0, -1.0, 1.0)


K, T, J, R, C, O, N, U = 512, 1024, 256, 512, 512, 256, 256, 128


def setup_inputs():
    n = np.random.standard_normal
    idx = np.random.permutation(T)[:J]
    idx2 = np.random.permutation(C)[:J]
    idx3 = np.random.permutation(C)[:C]
    idx4 = np.random.permutation(C)[:C]
    idx5 = np.random.permutation(C)[:O]
    idx6 = np.random.permutation(O)[:U]
    idx7 = np.random.permutation(O)[:U]
    fk = mx_kscale(K)
    fr = mx_kscale(R)
    xtp = pack_weight(n((K, T)) / fk[:, None], "e2m1")
    wp = pack_weight(n((K, R)) * 1 / np.sqrt(K) * fk[:, None], "e4m3")
    wbp = pack_weight(n((R, N)) * 1 / np.sqrt(R) / fr[:, None], "e2m1")
    return {
        "xt_words": xtp[0],
        "xt_scales": xtp[1],
        "w_words": wp[0],
        "w_scales": wp[1],
        "sa": (sgn((R, 1))).astype(np.float32),
        "sb": (np.random.uniform(0.5, 1.6, (R, 1)) * fr[:, None]).astype(np.float32),
        "sg": (sgn((R, 1))).astype(np.float32),
        "bg": (np.random.uniform(-2.0, 2.0, (R, 1))).astype(np.float32),
        "wb_words": wbp[0],
        "wb_scales": wbp[1],
        "so": (np.random.uniform(0.5, 1.6, (N, 1))).astype(np.float32),
        "sp": (np.random.uniform(0.5, 1.6, (N, 1))).astype(np.float32),
        "offs": striped(idx),
        "offs2": striped(idx2),
        "offs3": striped(idx3),
        "offs4": striped(idx4),
        "offs5": striped(idx5),
        "offs6": striped(idx6),
        "offs7": striped(idx7),
    }


def reference(xt_words, xt_scales, w_words, w_scales, sa, sb, sg, bg, wb_words, wb_scales, so, sp, offs, offs2, offs3, offs4, offs5, offs6, offs7):
    idx = unstriped(offs)
    idx2 = unstriped(offs2)
    idx3 = unstriped(offs3)
    idx4 = unstriped(offs4)
    idx5 = unstriped(offs5)
    idx6 = unstriped(offs6)
    idx7 = unstriped(offs7)
    xtu = unpack_weight(xt_words, xt_scales, "e2m1")
    wu = unpack_weight(w_words, w_scales, "e4m3")
    wbu = unpack_weight(wb_words, wb_scales, "e2m1")
    xtidxg = xtu[:, idx]
    a = wu.T @ xtidxg
    pw = np.zeros((R, C))
    pw[:, idx2] = a
    pg = np.maximum(pw, pw[:, idx3] * f64(sa) * sigmoid(pw[:, idx4] * f64(sg) + f64(bg)))
    hid = pg[:, idx5] * f64(sb)
    hidq = mxq(hid, 0, "e5m2")
    p = wbu.T @ hidq
    y = np.maximum(p[:, idx6] * f64(so), p[:, idx7] * f64(sp))
    return y

@@ -1,0 +1,199 @@
+from contextlib import ExitStack
+
+import concourse.mybir as mybir
+
+K, T, J, R, C, O, N, U = 512, 1024, 256, 512, 512, 256, 256, 128
+FLOPS = 2 * K * R * J + 2 * R * N * O
+
+F32 = mybir.dt.float32
+BF16 = mybir.dt.bfloat16
+I32 = mybir.dt.int32
+U32 = mybir.dt.uint32
+U16 = mybir.dt.uint16
+U8 = mybir.dt.uint8
+E4M3X4 = mybir.dt.float8_e4m3fn_x4
+E5M2X4 = mybir.dt.float8_e5m2_x4
+E2M1X4 = mybir.dt.float4_e2m1fn_x4
+COPY = mybir.ActivationFunctionType.Copy
+SIGMOID = mybir.ActivationFunctionType.Sigmoid
+MULT = mybir.AluOpType.mult
+MAX = mybir.AluOpType.max
+
+P = 128
+PACK = 4
+QUADS = 4
+QUAD = 32
+LIST = 16
+
+
+def tile_list_gatedladder_solo_one_pairweighed_kernel(
+    tc, xt_words, xt_scales, w_words, w_scales, sa, sb, sg, bg, wb_words, wb_scales, so, sp,
+    offs, offs2, offs3, offs4, offs5, offs6, offs7, out,
+):
+    nc = tc.nc
+
+    def entries(lst, first, count):
+        return lst[:, first // LIST : (first + count) // LIST]
+
+    with ExitStack() as ctx:
+        keep = ctx.enter_context(tc.tile_pool(name="keep", bufs=1))
+        psum = ctx.enter_context(tc.psum_pool(name="psum", bufs=1))
+
+        def load_list(src, name):
+            lst = keep.tile([P, src.shape[1]], U16, name=name)
+            nc.sync.dma_start(lst[:], src)
+            return lst
+
+        def load_scale_rows(queue, plane, scales, q):
+            queue.dma_start(
+                out=plane[QUAD * q : QUAD * q + PACK, :].bitcast(I32),
+                in_=scales[0, PACK * q : PACK * (q + 1), :].bitcast(I32),
+            )
+
+        def load_rowwise(src, name):
+            vec = keep.tile([P, PACK], F32, name=name)
+            nc.sync.dma_start(out=vec[:], in_=src.rearrange("(p t) one -> p (t one)", t=PACK))
+            return vec
+
+        xs = keep.tile([P, T], U8, name="xs")
+        nc.vector.memset(xs[:].bitcast(I32), 0)
+        ws = keep.tile([P, R], U8, name="ws")
+        nc.vector.memset(ws[:].bitcast(I32), 0)
+        pw = [keep.tile([P, 2 * C], F32, name="pw%d" % t) for t in range(PACK)]
+        for t in range(PACK):
+            (nc.vector if t < 2 else nc.gpsimd).memset(pw[t][:, :C], 0.0)
+        wbs = keep.tile([P, N], U8, name="wbs", align_bytes=64)
+        nc.gpsimd.memset(wbs[:].bitcast(I32), 0)
+
+        l1 = load_list(offs, "l1")
+        xw = keep.tile([P, T], U16, name="xw")
+        nc.sync.dma_start(out=xw[:].bitcast(I32), in_=xt_words[0].bitcast(I32))
+        ws_rows = keep.tile([PACK, QUADS, R // 4], I32, name="ws_rows")
+        nc.scalar.dma_start(out=ws_rows[:], in_=w_scales[0].bitcast(I32).rearrange("(q r) c -> r q c", r=PACK))
+        ww = keep.tile([P, R], U32, name="ww")
+        nc.scalar.dma_start(out=ww[:].bitcast(I32), in_=w_words[0].rearrange("p c b -> p (c b)").bitcast(I32))
+        for q in range(QUADS):
+            load_scale_rows(nc.sync if q < 2 else nc.scalar, xs, xt_scales, q)
+        l2 = load_list(offs2, "l2")
+        l4 = load_list(offs4, "l4")
+        sg_t = load_rowwise(sg, "sg_t")
+        bg_t = load_rowwise(bg, "bg_t")
+        l3 = load_list(offs3, "l3")
+        sa_t = load_rowwise(sa, "sa_t")
+        l5 = load_list(offs5, "l5")
+        sb_t = load_rowwise(sb, "sb_t")
+        wbw = keep.tile([P, 2 * N], U8, name="wbw", align_bytes=64)
+        nc.sync.dma_start(out=wbw[:].bitcast(I32), in_=wb_words[0].bitcast(I32))
+        for q in range(QUADS):
+            load_scale_rows(nc.sync, wbs, wb_scales, q)
+        l6 = load_list(offs6, "l6")
+        l7 = load_list(offs7, "l7")
+        so_t = keep.tile([P, N // P], F32, name="so_t")
+        sp_t = keep.tile([P, N // P], F32, name="sp_t")
+        with nc.allow_non_contiguous_dma(reason="one float32 weight for each partition and output tile"):
+            nc.sync.dma_start(out=so_t[:], in_=so.rearrange("(m p) one -> p (m one)", p=P))
+            nc.sync.dma_start(out=sp_t[:], in_=sp.rearrange("(m p) one -> p (m one)", p=P))
+
+        for q in range(QUADS):
+            nc.vector.tensor_copy(out=ws[QUAD * q : QUAD * q + PACK, :].bitcast(I32), in_=ws_rows[:, q, :])
+        ws_by_t = ws[:].rearrange("p (m t) -> p t m", t=PACK)
+        ww_by_t = ww[:].rearrange("p (m t) -> p t m", t=PACK)
+        wsd0 = keep.tile([P, P], U8, name="wsd0", align_bytes=64)
+        wsd = keep.tile([P, PACK - 1, P], U8, name="wsd", align_bytes=64)
+        wwd0 = keep.tile([P, P], U32, name="wwd0", align_bytes=64)
+        wwd = keep.tile([P, PACK - 1, P], U32, name="wwd", align_bytes=64)
+        nc.scalar.copy(out=wwd0[:], in_=ww_by_t[:, 0, :])
+        nc.scalar.copy(out=wwd[:], in_=ww_by_t[:, 1:, :])
+        w_codes = [wwd0[:]] + [wwd[:, t, :] for t in range(PACK - 1)]
+        w_bytes = [wsd0[:]] + [wsd[:, t, :] for t in range(PACK - 1)]
+
+        H = J // 2
+        xsg = keep.tile([P, J], U8, name="xsg", align_bytes=64)
+        xwg = keep.tile([P, J], U16, name="xwg", align_bytes=64)
+        a_sb = [keep.tile([P, J], F32, name="a_sb%d" % t) for t in range(PACK)]
+
+        def first_matmul(acc, t, cols):
+            nc.tensor.matmul_mx(
+                out=acc, lhsT=w_codes[t].bitcast(E4M3X4), lhsT_scale=w_bytes[t],
+                rhs=xwg[:, cols].bitcast(E2M1X4), rhs_scale=xsg[:, cols], start=True, stop=True,
+            )
+
+        for h in range(2):
+            cols = slice(h * H, (h + 1) * H)
+            nc.vector.tensor_copy(out=xsg[:, cols], in_=xs[:].indirect(entries(l1, h * H, H)))
+            if h == 0:
+                nc.vector.tensor_copy(out=wsd0[:], in_=ws_by_t[:, 0, :])
+            nc.vector.tensor_copy(out=xwg[:, cols], in_=xw[:].indirect(entries(l1, h * H, H)))
+            acc = psum.tile([P, H], F32, name="a0_%d" % h)
+            first_matmul(acc[:], 0, cols)
+            if h == 0:
+                nc.scalar.copy(out=a_sb[0][:, cols], in_=acc[:])
+            else:
+                nc.vector.tensor_copy(out=a_sb[0][:, cols], in_=acc[:])
+            nc.scalar.activation(out=pw[0][:].indirect(entries(l2, h * H, H)), in_=a_sb[0][:, cols], func=COPY)
+        nc.gpsimd.tensor_copy(out=wsd[:], in_=ws_by_t[:, 1:, :])
+        for t in range(1, PACK):
+            acc = psum.tile([P, J], F32, name="a%d" % t)
+            first_matmul(acc[:], t, slice(0, J))
+            nc.vector.tensor_copy(out=a_sb[t][:], in_=acc[:])
+            nc.vector.tensor_copy(out=pw[t][:].indirect(l2[:]), in_=a_sb[t][:])
+
+        pg = [keep.tile([P, C], F32, name="pg%d" % t) for t in range(PACK)]
+        for t in range(PACK):
+            gate = keep.tile([P, C], F32, name="gate%d" % t)
+            val = keep.tile([P, C], F32, name="val%d" % t)
+            prod = keep.tile([P, C], F32, name="prod%d" % t)
+            nc.scalar.activation(
+                out=gate[:], in_=pw[t][:].indirect(l4[:]), func=SIGMOID,
+                bias=bg_t[:, t : t + 1], scale=sg_t[:, t : t + 1],
+            )
+            nc.scalar.activation(out=val[:], in_=pw[t][:].indirect(l3[:]), func=COPY, scale=sa_t[:, t : t + 1])
+            nc.vector.tensor_tensor(out=prod[:], in0=val[:], in1=gate[:], op=MULT)
+            nc.vector.tensor_tensor(out=pg[t][:], in0=pw[t][:, :C], in1=prod[:], op=MAX)
+
+        D = O // 2
+        p_sb = [keep.tile([P, O], F32, name="p_sb%d" % m) for m in range(N // P)]
+        hid = [keep.tile([P, PACK, D], F32, name="hid%d" % h) for h in range(2)]
+
+        def pick(h, t):
+            nc.scalar.activation(
+                out=hid[h][:, t, :], in_=pg[t][:].indirect(entries(l5, h * D, D)), func=COPY, scale=sb_t[:, t : t + 1],
+            )
+
+        def second_stage(h):
+            woven = keep.tile([P, D, PACK], BF16, name="woven%d" % h, align_bytes=64)
+            nc.vector.tensor_copy(out=woven[:], in_=hid[h][:].rearrange("p t o -> p o t"))
+            codes = keep.tile([P, D], U32, name="codes%d" % h, align_bytes=64)
+            bytes_h = keep.tile([P, D], U8, name="hs%d" % h, align_bytes=64)
+            nc.vector.quantize_mx(out=codes[:].bitcast(E5M2X4), scales=bytes_h[:], in_=woven[:].rearrange("p o t -> p (o t)"))
+            accs = []
+            for m in range(N // P):
+                acc = psum.tile([P, D], F32, name="p%d_%d" % (h, m) if h == 1 else "a0_%d" % m)
+                nc.tensor.matmul_mx(
+                    out=acc[:], lhsT=wbw[:, 2 * P * m : 2 * P * (m + 1)].bitcast(E2M1X4), lhsT_scale=wbs[:, P * m : P * (m + 1)],
+                    rhs=codes[:].bitcast(E5M2X4), rhs_scale=bytes_h[:], start=True, stop=True,
+                )
+                accs.append(acc)
+            return accs
+
+        for t in range(PACK - 1):
+            pick(0, t)
+        pick(1, 0)
+        pick(0, PACK - 1)
+        first = second_stage(0)
+        for t in range(1, PACK):
+            pick(1, t)
+        second = second_stage(1)
+        for m in range(N // P):
+            nc.scalar.copy(out=p_sb[m][:, :D], in_=first[m][:])
+        nc.scalar.copy(out=p_sb[0][:, D:], in_=second[0][:])
+        nc.vector.tensor_copy(out=p_sb[1][:, D:], in_=second[1][:])
+
+        for m in range(N // P):
+            left = keep.tile([P, U], F32, name="left%d" % m)
+            right = keep.tile([P, U], F32, name="right%d" % m)
+            y = keep.tile([P, U], F32, name="y%d" % m)
+            nc.scalar.activation(out=left[:], in_=p_sb[m][:].indirect(l6[:]), func=COPY, scale=so_t[:, m : m + 1])
+            nc.scalar.activation(out=right[:], in_=p_sb[m][:].indirect(l7[:]), func=COPY, scale=sp_t[:, m : m + 1])
+            nc.vector.tensor_tensor(out=y[:], in0=left[:], in1=right[:], op=MAX)
+            nc.sync.dma_start(out=out[P * m : P * (m + 1), :], in_=y[:])

@@ -57,6 +57,8 @@ def tile_list_gatedladder_solo_one_pairweighed_kernel(
 
         xs = keep.tile([P, T], U8, name="xs")
         nc.vector.memset(xs[:].bitcast(I32), 0)
+        warm = keep.tile([P, 2], F32, name="warm")
+        nc.vector.memset(warm[:, 0:1], 0.0)
         ws = keep.tile([P, R], U8, name="ws")
         nc.vector.memset(ws[:].bitcast(I32), 0)
         pw = [keep.tile([P, 2 * C], F32, name="pw%d" % t) for t in range(PACK)]
@@ -74,6 +76,7 @@ def tile_list_gatedladder_solo_one_pairweighed_kernel(
         nc.scalar.dma_start(out=ww[:].bitcast(I32), in_=w_words[0].rearrange("p c b -> p (c b)").bitcast(I32))
         for q in range(QUADS):
             load_scale_rows(nc.sync if q < 2 else nc.scalar, xs, xt_scales, q)
+        nc.scalar.activation(out=warm[:, 1:2], in_=warm[:, 0:1], func=SIGMOID)
         l2 = load_list(offs2, "l2")
         l4 = load_list(offs4, "l4")
         sg_t = load_rowwise(sg, "sg_t")

@@ -63,9 +63,9 @@ def tile_list_gatedladder_solo_one_pairweighed_kernel(
         nc.vector.memset(ws[:].bitcast(I32), 0)
         pw = [keep.tile([P, 2 * C], F32, name="pw%d" % t) for t in range(PACK)]
         for t in range(PACK):
-            (nc.vector if t < 2 else nc.gpsimd).memset(pw[t][:, :C], 0.0)
+            nc.vector.memset(pw[t][:, :C].bitcast(I32), 0)
         wbs = keep.tile([P, N], U8, name="wbs", align_bytes=64)
-        nc.gpsimd.memset(wbs[:].bitcast(I32), 0)
+        nc.vector.memset(wbs[:].bitcast(I32), 0)
 
         l1 = load_list(offs, "l1")
         xw = keep.tile([P, T], U16, name="xw")
@@ -102,13 +102,12 @@ def tile_list_gatedladder_solo_one_pairweighed_kernel(
         ws_by_t = ws[:].rearrange("p (m t) -> p t m", t=PACK)
         ww_by_t = ww[:].rearrange("p (m t) -> p t m", t=PACK)
         wsd0 = keep.tile([P, P], U8, name="wsd0", align_bytes=64)
-        wsd = keep.tile([P, PACK - 1, P], U8, name="wsd", align_bytes=64)
         wwd0 = keep.tile([P, P], U32, name="wwd0", align_bytes=64)
         wwd = keep.tile([P, PACK - 1, P], U32, name="wwd", align_bytes=64)
         nc.scalar.copy(out=wwd0[:], in_=ww_by_t[:, 0, :])
-        nc.scalar.copy(out=wwd[:], in_=ww_by_t[:, 1:, :])
+        nc.scalar.copy(out=wwd[:].rearrange("p t m -> p m t"), in_=ww[:].rearrange("p (m t) -> p m t", t=PACK)[:, :, 1:])
         w_codes = [wwd0[:]] + [wwd[:, t, :] for t in range(PACK - 1)]
-        w_bytes = [wsd0[:]] + [wsd[:, t, :] for t in range(PACK - 1)]
+        w_bytes = [wsd0[:]]
 
         H = J // 2
         xsg = keep.tile([P, J], U8, name="xsg", align_bytes=64)
@@ -132,9 +131,11 @@ def tile_list_gatedladder_solo_one_pairweighed_kernel(
             if h == 0:
                 nc.scalar.copy(out=a_sb[0][:, cols], in_=acc[:])
             else:
+                wsd = keep.tile([P, PACK - 1, P], U8, name="wsd", align_bytes=64)
+                nc.vector.tensor_copy(out=wsd[:], in_=ws_by_t[:, 1:, :])
+                w_bytes.extend(wsd[:, t, :] for t in range(PACK - 1))
                 nc.vector.tensor_copy(out=a_sb[0][:, cols], in_=acc[:])
             nc.scalar.activation(out=pw[0][:].indirect(entries(l2, h * H, H)), in_=a_sb[0][:, cols], func=COPY)
-        nc.gpsimd.tensor_copy(out=wsd[:], in_=ws_by_t[:, 1:, :])
         for t in range(1, PACK):
             acc = psum.tile([P, J], F32, name="a%d" % t)
             first_matmul(acc[:], t, slice(0, J))
@@ -150,9 +151,14 @@ def tile_list_gatedladder_solo_one_pairweighed_kernel(
                 out=gate[:], in_=pw[t][:].indirect(l4[:]), func=SIGMOID,
                 bias=bg_t[:, t : t + 1], scale=sg_t[:, t : t + 1],
             )
-            nc.scalar.activation(out=val[:], in_=pw[t][:].indirect(l3[:]), func=COPY, scale=sa_t[:, t : t + 1])
-            nc.vector.tensor_tensor(out=prod[:], in0=val[:], in1=gate[:], op=MULT)
-            nc.vector.tensor_tensor(out=pg[t][:], in0=pw[t][:, :C], in1=prod[:], op=MAX)
+            width = C // 2 if t == PACK - 1 else C
+            for c0 in range(0, C, width):
+                cols = slice(c0, c0 + width)
+                nc.scalar.activation(
+                    out=val[:, cols], in_=pw[t][:].indirect(entries(l3, c0, width)), func=COPY, scale=sa_t[:, t : t + 1],
+                )
+                nc.vector.tensor_tensor(out=prod[:, cols], in0=val[:, cols], in1=gate[:, cols], op=MULT)
+                nc.vector.tensor_tensor(out=pg[t][:, cols], in0=pw[t][:, cols], in1=prod[:, cols], op=MAX)
 
         D = O // 2
         p_sb = [keep.tile([P, O], F32, name="p_sb%d" % m) for m in range(N // P)]
@@ -165,7 +171,9 @@ def tile_list_gatedladder_solo_one_pairweighed_kernel(
 
         def second_stage(h):
             woven = keep.tile([P, D, PACK], BF16, name="woven%d" % h, align_bytes=64)
-            nc.vector.tensor_copy(out=woven[:], in_=hid[h][:].rearrange("p t o -> p o t"))
+            nc.vector.tensor_copy(
+                out=woven[:].rearrange("p (c i) t -> p c t i", i=4), in_=hid[h][:].rearrange("p t (c i) -> p c t i", i=4),
+            )
             codes = keep.tile([P, D], U32, name="codes%d" % h, align_bytes=64)
             bytes_h = keep.tile([P, D], U8, name="hs%d" % h, align_bytes=64)
             nc.vector.quantize_mx(out=codes[:].bitcast(E5M2X4), scales=bytes_h[:], in_=woven[:].rearrange("p o t -> p (o t)"))

@@ -55,7 +55,7 @@ def tile_list_gatedladder_solo_one_pairweighed_kernel(
             nc.sync.dma_start(out=vec[:], in_=src.rearrange("(p t) one -> p (t one)", t=PACK))
             return vec
 
-        xs = keep.tile([P, T], U8, name="xs")
+        xs = keep.tile([P, T], U8, name="xs", tag="xs", align_bytes=64)
         nc.vector.memset(xs[:].bitcast(I32), 0)
         warm = keep.tile([P, 2], F32, name="warm")
         nc.vector.memset(warm[:, 0:1], 0.0)
@@ -67,22 +67,22 @@ def tile_list_gatedladder_solo_one_pairweighed_kernel(
         wbs = keep.tile([P, N], U8, name="wbs", align_bytes=64)
         nc.vector.memset(wbs[:].bitcast(I32), 0)
 
-        l1 = load_list(offs, "l1")
+        ws_rows = keep.tile([PACK, QUADS, R // 4], I32, name="ws_rows")
+        nc.sync.dma_start(out=ws_rows[:], in_=w_scales[0].bitcast(I32).rearrange("(q r) c -> r q c", r=PACK))
         xw = keep.tile([P, T], U16, name="xw")
         nc.sync.dma_start(out=xw[:].bitcast(I32), in_=xt_words[0].bitcast(I32))
-        ws_rows = keep.tile([PACK, QUADS, R // 4], I32, name="ws_rows")
-        nc.scalar.dma_start(out=ws_rows[:], in_=w_scales[0].bitcast(I32).rearrange("(q r) c -> r q c", r=PACK))
+        l1 = load_list(offs, "l1")
         ww = keep.tile([P, R], U32, name="ww")
         nc.scalar.dma_start(out=ww[:].bitcast(I32), in_=w_words[0].rearrange("p c b -> p (c b)").bitcast(I32))
         for q in range(QUADS):
-            load_scale_rows(nc.sync if q < 2 else nc.scalar, xs, xt_scales, q)
+            load_scale_rows(nc.sync, xs, xt_scales, q)
         nc.scalar.activation(out=warm[:, 1:2], in_=warm[:, 0:1], func=SIGMOID)
         l2 = load_list(offs2, "l2")
         l4 = load_list(offs4, "l4")
-        sg_t = load_rowwise(sg, "sg_t")
-        bg_t = load_rowwise(bg, "bg_t")
         l3 = load_list(offs3, "l3")
+        sg_t = load_rowwise(sg, "sg_t")
         sa_t = load_rowwise(sa, "sa_t")
+        bg_t = load_rowwise(bg, "bg_t")
         l5 = load_list(offs5, "l5")
         sb_t = load_rowwise(sb, "sb_t")
         wbw = keep.tile([P, 2 * N], U8, name="wbw", align_bytes=64)
@@ -112,7 +112,7 @@ def tile_list_gatedladder_solo_one_pairweighed_kernel(
         H = J // 2
         xsg = keep.tile([P, J], U8, name="xsg", align_bytes=64)
         xwg = keep.tile([P, J], U16, name="xwg", align_bytes=64)
-        a_sb = [keep.tile([P, J], F32, name="a_sb%d" % t) for t in range(PACK)]
+        a_sb = keep.tile([P, PACK, J], F32, name="a_sb", tag="a_then_prod")
 
         def first_matmul(acc, t, cols):
             nc.tensor.matmul_mx(
@@ -120,45 +120,68 @@ def tile_list_gatedladder_solo_one_pairweighed_kernel(
                 rhs=xwg[:, cols].bitcast(E2M1X4), rhs_scale=xsg[:, cols], start=True, stop=True,
             )
 
+        nc.vector.tensor_copy(out=xwg[:], in_=xw[:].indirect(l1[:]))
+        nc.vector.tensor_copy(out=wsd0[:], in_=ws_by_t[:, 0, :])
         for h in range(2):
             cols = slice(h * H, (h + 1) * H)
             nc.vector.tensor_copy(out=xsg[:, cols], in_=xs[:].indirect(entries(l1, h * H, H)))
-            if h == 0:
-                nc.vector.tensor_copy(out=wsd0[:], in_=ws_by_t[:, 0, :])
-            nc.vector.tensor_copy(out=xwg[:, cols], in_=xw[:].indirect(entries(l1, h * H, H)))
             acc = psum.tile([P, H], F32, name="a0_%d" % h)
             first_matmul(acc[:], 0, cols)
             if h == 0:
-                nc.scalar.copy(out=a_sb[0][:, cols], in_=acc[:])
+                nc.scalar.copy(out=a_sb[:, 0, cols], in_=acc[:])
             else:
-                wsd = keep.tile([P, PACK - 1, P], U8, name="wsd", align_bytes=64)
+                wsd = keep.tile([P, PACK - 1, P], U8, name="wsd", tag="xs", align_bytes=64)
                 nc.vector.tensor_copy(out=wsd[:], in_=ws_by_t[:, 1:, :])
                 w_bytes.extend(wsd[:, t, :] for t in range(PACK - 1))
-                nc.vector.tensor_copy(out=a_sb[0][:, cols], in_=acc[:])
-            nc.scalar.activation(out=pw[0][:].indirect(entries(l2, h * H, H)), in_=a_sb[0][:, cols], func=COPY)
+                nc.vector.tensor_copy(out=a_sb[:, 0, cols], in_=acc[:])
+            nc.scalar.activation(out=pw[0][:].indirect(entries(l2, h * H, H)), in_=a_sb[:, 0, cols], func=COPY)
+        for first, count in ((1, 2), (3, 1)):
+            acc = psum.tile([P, count, J], F32, name="a%d" % first)
+            for i in range(count):
+                first_matmul(acc[:, i, :], first + i, slice(0, J))
+            nc.vector.tensor_copy(out=a_sb[:, first : first + count, :], in_=acc[:])
         for t in range(1, PACK):
-            acc = psum.tile([P, J], F32, name="a%d" % t)
-            first_matmul(acc[:], t, slice(0, J))
-            nc.vector.tensor_copy(out=a_sb[t][:], in_=acc[:])
-            nc.vector.tensor_copy(out=pw[t][:].indirect(l2[:]), in_=a_sb[t][:])
+            nc.vector.tensor_copy(out=pw[t][:].indirect(l2[:]), in_=a_sb[:, t, :])
 
         pg = [keep.tile([P, C], F32, name="pg%d" % t) for t in range(PACK)]
-        for t in range(PACK):
-            gate = keep.tile([P, C], F32, name="gate%d" % t)
-            val = keep.tile([P, C], F32, name="val%d" % t)
-            prod = keep.tile([P, C], F32, name="prod%d" % t)
+        gate = keep.tile([P, PACK * C], F32, name="gate")
+        val = keep.tile([P, PACK * C], F32, name="val")
+        prod = keep.tile([P, PACK * C], F32, name="prod", tag="a_then_prod")
+
+        def fetch_gate(t):
             nc.scalar.activation(
-                out=gate[:], in_=pw[t][:].indirect(l4[:]), func=SIGMOID,
+                out=gate[:, t * C : (t + 1) * C], in_=pw[t][:].indirect(l4[:]), func=SIGMOID,
                 bias=bg_t[:, t : t + 1], scale=sg_t[:, t : t + 1],
             )
-            width = C // 2 if t == PACK - 1 else C
+
+        def fetch_val(t, c0, width):
+            nc.scalar.activation(
+                out=val[:, t * C + c0 : t * C + c0 + width], in_=pw[t][:].indirect(entries(l3, c0, width)),
+                func=COPY, scale=sa_t[:, t : t + 1],
+            )
+
+        def multiply(start, width):
+            run = slice(start, start + width)
+            nc.vector.tensor_tensor(out=prod[:, run], in0=val[:, run], in1=gate[:, run], op=MULT)
+
+        def keep_larger(t, c0, width):
+            nc.vector.tensor_tensor(
+                out=pg[t][:, c0 : c0 + width], in0=pw[t][:, c0 : c0 + width],
+                in1=prod[:, t * C + c0 : t * C + c0 + width], op=MAX,
+            )
+
+        for t in range(2):
+            fetch_gate(t)
+            fetch_val(t, 0, C)
+        multiply(0, 2 * C)
+        for t in range(2):
+            keep_larger(t, 0, C)
+        for t, width in ((2, C), (3, C // 2)):
+            fetch_gate(t)
             for c0 in range(0, C, width):
-                cols = slice(c0, c0 + width)
-                nc.scalar.activation(
-                    out=val[:, cols], in_=pw[t][:].indirect(entries(l3, c0, width)), func=COPY, scale=sa_t[:, t : t + 1],
-                )
-                nc.vector.tensor_tensor(out=prod[:, cols], in0=val[:, cols], in1=gate[:, cols], op=MULT)
-                nc.vector.tensor_tensor(out=pg[t][:, cols], in0=pw[t][:, cols], in1=prod[:, cols], op=MAX)
+                fetch_val(t, c0, width)
+                multiply(t * C + c0, width)
+                keep_larger(t, c0, width)
 
         D = O // 2
         p_sb = [keep.tile([P, O], F32, name="p_sb%d" % m) for m in range(N // P)]

@@ -22,8 +22,14 @@ MAX = mybir.AluOpType.max
 P = 128
 PACK = 4
 QUADS = 4
-QUAD = 32
+QUAD = P // QUADS
+ROWS = 4
 LIST = 16
+MX_ALIGN = 64
+M_TILES = N // P
+HALF_J = J // 2
+HALF_O = O // 2
+LINE = 4
 
 
 def tile_list_gatedladder_solo_one_pairweighed_kernel(
@@ -44,101 +50,110 @@ def tile_list_gatedladder_solo_one_pairweighed_kernel(
             nc.sync.dma_start(lst[:], src)
             return lst
 
-        def load_scale_rows(queue, plane, scales, q):
-            queue.dma_start(
-                out=plane[QUAD * q : QUAD * q + PACK, :].bitcast(I32),
-                in_=scales[0, PACK * q : PACK * (q + 1), :].bitcast(I32),
-            )
+        def load_scale_plane(plane, scales):
+            for q in range(QUADS):
+                nc.sync.dma_start(
+                    out=plane[QUAD * q : QUAD * q + ROWS, :].bitcast(I32),
+                    in_=scales[0, ROWS * q : ROWS * (q + 1), :].bitcast(I32),
+                )
 
-        def load_rowwise(src, name):
+        def load_by_slice(src, name):
             vec = keep.tile([P, PACK], F32, name=name)
             nc.sync.dma_start(out=vec[:], in_=src.rearrange("(p t) one -> p (t one)", t=PACK))
             return vec
 
-        xs = keep.tile([P, T], U8, name="xs", tag="xs", align_bytes=64)
+        def zeroed_board(t, **place):
+            board = keep.tile([P, 2 * C], F32, name="pw%d" % t, **place)
+            nc.vector.memset(board[:, :C].bitcast(I32), 0)
+            return board
+
+        xs = keep.tile([P, T], U8, name="xs", tag="xs", align_bytes=MX_ALIGN)
         nc.vector.memset(xs[:].bitcast(I32), 0)
         warm = keep.tile([P, 2], F32, name="warm")
         nc.vector.memset(warm[:, 0:1], 0.0)
         ws = keep.tile([P, R], U8, name="ws")
         nc.vector.memset(ws[:].bitcast(I32), 0)
-        pw = [keep.tile([P, 2 * C], F32, name="pw%d" % t) for t in range(PACK)]
-        for t in range(PACK):
-            nc.vector.memset(pw[t][:, :C].bitcast(I32), 0)
-        wbs = keep.tile([P, N], U8, name="wbs", align_bytes=64)
+        pw = [zeroed_board(t) for t in range(PACK - 1)]
+        wbs = keep.tile([P, N], U8, name="wbs", align_bytes=MX_ALIGN)
         nc.vector.memset(wbs[:].bitcast(I32), 0)
 
-        ws_rows = keep.tile([PACK, QUADS, R // 4], I32, name="ws_rows")
-        nc.sync.dma_start(out=ws_rows[:], in_=w_scales[0].bitcast(I32).rearrange("(q r) c -> r q c", r=PACK))
+        ws_rows = keep.tile([ROWS, QUADS, R // 4], I32, name="ws_rows")
+        nc.sync.dma_start(out=ws_rows[:], in_=w_scales[0].bitcast(I32).rearrange("(q r) c -> r q c", r=ROWS))
         xw = keep.tile([P, T], U16, name="xw")
         nc.sync.dma_start(out=xw[:].bitcast(I32), in_=xt_words[0].bitcast(I32))
         l1 = load_list(offs, "l1")
         ww = keep.tile([P, R], U32, name="ww")
         nc.scalar.dma_start(out=ww[:].bitcast(I32), in_=w_words[0].rearrange("p c b -> p (c b)").bitcast(I32))
-        for q in range(QUADS):
-            load_scale_rows(nc.sync, xs, xt_scales, q)
+        load_scale_plane(xs, xt_scales)
         nc.scalar.activation(out=warm[:, 1:2], in_=warm[:, 0:1], func=SIGMOID)
         l2 = load_list(offs2, "l2")
         l4 = load_list(offs4, "l4")
         l3 = load_list(offs3, "l3")
-        sg_t = load_rowwise(sg, "sg_t")
-        sa_t = load_rowwise(sa, "sa_t")
-        bg_t = load_rowwise(bg, "bg_t")
+        sg_t = load_by_slice(sg, "sg_t")
+        sa_t = load_by_slice(sa, "sa_t")
+        bg_t = load_by_slice(bg, "bg_t")
         l5 = load_list(offs5, "l5")
-        sb_t = load_rowwise(sb, "sb_t")
-        wbw = keep.tile([P, 2 * N], U8, name="wbw", align_bytes=64)
+        sb_t = load_by_slice(sb, "sb_t")
+        wbw = keep.tile([P, 2 * N], U8, name="wbw", align_bytes=MX_ALIGN)
         nc.sync.dma_start(out=wbw[:].bitcast(I32), in_=wb_words[0].bitcast(I32))
-        for q in range(QUADS):
-            load_scale_rows(nc.sync, wbs, wb_scales, q)
+        load_scale_plane(wbs, wb_scales)
         l6 = load_list(offs6, "l6")
         l7 = load_list(offs7, "l7")
-        so_t = keep.tile([P, N // P], F32, name="so_t")
-        sp_t = keep.tile([P, N // P], F32, name="sp_t")
+        so_t = keep.tile([P, M_TILES], F32, name="so_t")
+        sp_t = keep.tile([P, M_TILES], F32, name="sp_t")
         with nc.allow_non_contiguous_dma(reason="one float32 weight for each partition and output tile"):
             nc.sync.dma_start(out=so_t[:], in_=so.rearrange("(m p) one -> p (m one)", p=P))
             nc.sync.dma_start(out=sp_t[:], in_=sp.rearrange("(m p) one -> p (m one)", p=P))
 
         for q in range(QUADS):
-            nc.vector.tensor_copy(out=ws[QUAD * q : QUAD * q + PACK, :].bitcast(I32), in_=ws_rows[:, q, :])
-        ws_by_t = ws[:].rearrange("p (m t) -> p t m", t=PACK)
-        ww_by_t = ww[:].rearrange("p (m t) -> p t m", t=PACK)
-        wsd0 = keep.tile([P, P], U8, name="wsd0", align_bytes=64)
-        wwd0 = keep.tile([P, P], U32, name="wwd0", align_bytes=64)
-        wwd = keep.tile([P, PACK - 1, P], U32, name="wwd", align_bytes=64)
-        nc.scalar.copy(out=wwd0[:], in_=ww_by_t[:, 0, :])
-        nc.scalar.copy(out=wwd[:].rearrange("p t m -> p m t"), in_=ww[:].rearrange("p (m t) -> p m t", t=PACK)[:, :, 1:])
-        w_codes = [wwd0[:]] + [wwd[:, t, :] for t in range(PACK - 1)]
-        w_bytes = [wsd0[:]]
+            nc.vector.tensor_copy(out=ws[QUAD * q : QUAD * q + ROWS, :].bitcast(I32), in_=ws_rows[:, q, :])
+        ws_by_slice = ws[:].rearrange("p (m t) -> p t m", t=PACK)
+        ww_by_column = ww[:].rearrange("p (m t) -> p m t", t=PACK)
+        wsd0 = keep.tile([P, P], U8, name="wsd0", align_bytes=MX_ALIGN)
+        wwd0 = keep.tile([P, P], U32, name="wwd0", tag="wwd0", align_bytes=MX_ALIGN)
+        wwd = keep.tile([P, PACK - 1, P], U32, name="wwd", align_bytes=MX_ALIGN)
+        nc.scalar.copy(out=wwd0[:], in_=ww_by_column[:, :, 0])
+        nc.scalar.copy(out=wwd[:].rearrange("p t m -> p m t"), in_=ww_by_column[:, :, 1:])
 
-        H = J // 2
-        xsg = keep.tile([P, J], U8, name="xsg", align_bytes=64)
-        xwg = keep.tile([P, J], U16, name="xwg", align_bytes=64)
+        xsg = keep.tile([P, J], U8, name="xsg", align_bytes=MX_ALIGN)
+        xwg = keep.tile([P, J], U16, name="xwg", align_bytes=MX_ALIGN)
         a_sb = keep.tile([P, PACK, J], F32, name="a_sb", tag="a_then_prod")
 
-        def first_matmul(acc, t, cols):
+        def first_matmul(acc, words, scale_bytes, slots):
             nc.tensor.matmul_mx(
-                out=acc, lhsT=w_codes[t].bitcast(E4M3X4), lhsT_scale=w_bytes[t],
-                rhs=xwg[:, cols].bitcast(E2M1X4), rhs_scale=xsg[:, cols], start=True, stop=True,
+                out=acc, lhsT=words.bitcast(E4M3X4), lhsT_scale=scale_bytes,
+                rhs=xwg[:, slots].bitcast(E2M1X4), rhs_scale=xsg[:, slots], start=True, stop=True,
+            )
+
+        def slice0_half(h):
+            slots = slice(h * HALF_J, (h + 1) * HALF_J)
+            nc.vector.tensor_copy(out=xsg[:, slots], in_=xs[:].indirect(entries(l1, h * HALF_J, HALF_J)))
+            acc = psum.tile([P, HALF_J], F32, name="a0_%d" % h)
+            first_matmul(acc[:], wwd0[:], wsd0[:], slots)
+            return acc
+
+        def slice0_put(h):
+            nc.scalar.activation(
+                out=pw[0][:].indirect(entries(l2, h * HALF_J, HALF_J)),
+                in_=a_sb[:, 0, h * HALF_J : (h + 1) * HALF_J], func=COPY,
             )
 
         nc.vector.tensor_copy(out=xwg[:], in_=xw[:].indirect(l1[:]))
-        nc.vector.tensor_copy(out=wsd0[:], in_=ws_by_t[:, 0, :])
-        for h in range(2):
-            cols = slice(h * H, (h + 1) * H)
-            nc.vector.tensor_copy(out=xsg[:, cols], in_=xs[:].indirect(entries(l1, h * H, H)))
-            acc = psum.tile([P, H], F32, name="a0_%d" % h)
-            first_matmul(acc[:], 0, cols)
-            if h == 0:
-                nc.scalar.copy(out=a_sb[:, 0, cols], in_=acc[:])
-            else:
-                wsd = keep.tile([P, PACK - 1, P], U8, name="wsd", tag="xs", align_bytes=64)
-                nc.vector.tensor_copy(out=wsd[:], in_=ws_by_t[:, 1:, :])
-                w_bytes.extend(wsd[:, t, :] for t in range(PACK - 1))
-                nc.vector.tensor_copy(out=a_sb[:, 0, cols], in_=acc[:])
-            nc.scalar.activation(out=pw[0][:].indirect(entries(l2, h * H, H)), in_=a_sb[:, 0, cols], func=COPY)
+        nc.vector.tensor_copy(out=wsd0[:], in_=ws_by_slice[:, 0, :])
+        acc = slice0_half(0)
+        nc.scalar.copy(out=a_sb[:, 0, :HALF_J], in_=acc[:])
+        slice0_put(0)
+        acc = slice0_half(1)
+        wsd = keep.tile([P, PACK - 1, P], U8, name="wsd", tag="xs", align_bytes=MX_ALIGN)
+        nc.vector.tensor_copy(out=wsd[:], in_=ws_by_slice[:, 1:, :])
+        nc.vector.tensor_copy(out=a_sb[:, 0, HALF_J:], in_=acc[:])
+        slice0_put(1)
+        pw.append(zeroed_board(PACK - 1, tag="wwd0", align_bytes=MX_ALIGN))
+
         for first, count in ((1, 2), (3, 1)):
             acc = psum.tile([P, count, J], F32, name="a%d" % first)
             for i in range(count):
-                first_matmul(acc[:, i, :], first + i, slice(0, J))
+                first_matmul(acc[:, i, :], wwd[:, first + i - 1, :], wsd[:, first + i - 1, :], slice(0, J))
             nc.vector.tensor_copy(out=a_sb[:, first : first + count, :], in_=acc[:])
         for t in range(1, PACK):
             nc.vector.tensor_copy(out=pw[t][:].indirect(l2[:]), in_=a_sb[:, t, :])
@@ -183,47 +198,51 @@ def tile_list_gatedladder_solo_one_pairweighed_kernel(
                 multiply(t * C + c0, width)
                 keep_larger(t, c0, width)
 
-        D = O // 2
-        p_sb = [keep.tile([P, O], F32, name="p_sb%d" % m) for m in range(N // P)]
-        hid = [keep.tile([P, PACK, D], F32, name="hid%d" % h) for h in range(2)]
+        p_sb = [keep.tile([P, O], F32, name="p_sb%d" % m) for m in range(M_TILES)]
+        hid = [keep.tile([P, PACK, HALF_O], F32, name="hid%d" % h) for h in range(2)]
 
         def pick(h, t):
             nc.scalar.activation(
-                out=hid[h][:, t, :], in_=pg[t][:].indirect(entries(l5, h * D, D)), func=COPY, scale=sb_t[:, t : t + 1],
+                out=hid[h][:, t, :], in_=pg[t][:].indirect(entries(l5, h * HALF_O, HALF_O)),
+                func=COPY, scale=sb_t[:, t : t + 1],
             )
 
         def second_stage(h):
-            woven = keep.tile([P, D, PACK], BF16, name="woven%d" % h, align_bytes=64)
+            woven = keep.tile([P, HALF_O, PACK], BF16, name="woven%d" % h, align_bytes=MX_ALIGN)
             nc.vector.tensor_copy(
-                out=woven[:].rearrange("p (c i) t -> p c t i", i=4), in_=hid[h][:].rearrange("p t (c i) -> p c t i", i=4),
+                out=woven[:].rearrange("p (c i) t -> p c t i", i=LINE),
+                in_=hid[h][:].rearrange("p t (c i) -> p c t i", i=LINE),
             )
-            codes = keep.tile([P, D], U32, name="codes%d" % h, align_bytes=64)
-            bytes_h = keep.tile([P, D], U8, name="hs%d" % h, align_bytes=64)
-            nc.vector.quantize_mx(out=codes[:].bitcast(E5M2X4), scales=bytes_h[:], in_=woven[:].rearrange("p o t -> p (o t)"))
-            accs = []
-            for m in range(N // P):
-                acc = psum.tile([P, D], F32, name="p%d_%d" % (h, m) if h == 1 else "a0_%d" % m)
+            codes = keep.tile([P, HALF_O], U32, name="codes%d" % h, align_bytes=MX_ALIGN)
+            plane = keep.tile([P, HALF_O], U8, name="hs%d" % h, align_bytes=MX_ALIGN)
+            nc.vector.quantize_mx(
+                out=codes[:].bitcast(E5M2X4), scales=plane[:], in_=woven[:].rearrange("p o t -> p (o t)"),
+            )
+            sums = []
+            for m in range(M_TILES):
+                bank = psum.tile([P, HALF_O], F32, name=("a0_%d", "p1_%d")[h] % m)
                 nc.tensor.matmul_mx(
-                    out=acc[:], lhsT=wbw[:, 2 * P * m : 2 * P * (m + 1)].bitcast(E2M1X4), lhsT_scale=wbs[:, P * m : P * (m + 1)],
-                    rhs=codes[:].bitcast(E5M2X4), rhs_scale=bytes_h[:], start=True, stop=True,
+                    out=bank[:], lhsT=wbw[:, 2 * P * m : 2 * P * (m + 1)].bitcast(E2M1X4),
+                    lhsT_scale=wbs[:, P * m : P * (m + 1)],
+                    rhs=codes[:].bitcast(E5M2X4), rhs_scale=plane[:], start=True, stop=True,
                 )
-                accs.append(acc)
-            return accs
+                sums.append(bank)
+            return sums
 
         for t in range(PACK - 1):
             pick(0, t)
         pick(1, 0)
         pick(0, PACK - 1)
-        first = second_stage(0)
+        first_half = second_stage(0)
         for t in range(1, PACK):
             pick(1, t)
-        second = second_stage(1)
-        for m in range(N // P):
-            nc.scalar.copy(out=p_sb[m][:, :D], in_=first[m][:])
-        nc.scalar.copy(out=p_sb[0][:, D:], in_=second[0][:])
-        nc.vector.tensor_copy(out=p_sb[1][:, D:], in_=second[1][:])
+        second_half = second_stage(1)
+        for m in range(M_TILES):
+            nc.scalar.copy(out=p_sb[m][:, :HALF_O], in_=first_half[m][:])
+        nc.scalar.copy(out=p_sb[0][:, HALF_O:], in_=second_half[0][:])
+        nc.vector.tensor_copy(out=p_sb[1][:, HALF_O:], in_=second_half[1][:])
 
-        for m in range(N // P):
+        for m in range(M_TILES):
             left = keep.tile([P, U], F32, name="left%d" % m)
             right = keep.tile([P, U], F32, name="right%d" % m)
             y = keep.tile([P, U], F32, name="y%d" % m)

from contextlib import ExitStack

import concourse.mybir as mybir

K, T, J, R, C, O, N, U = 512, 1024, 256, 512, 512, 256, 256, 128
FLOPS = 2 * K * R * J + 2 * R * N * O

F32 = mybir.dt.float32
BF16 = mybir.dt.bfloat16
I32 = mybir.dt.int32
U32 = mybir.dt.uint32
U16 = mybir.dt.uint16
U8 = mybir.dt.uint8
E4M3X4 = mybir.dt.float8_e4m3fn_x4
E5M2X4 = mybir.dt.float8_e5m2_x4
E2M1X4 = mybir.dt.float4_e2m1fn_x4
COPY = mybir.ActivationFunctionType.Copy
SIGMOID = mybir.ActivationFunctionType.Sigmoid
MULT = mybir.AluOpType.mult
MAX = mybir.AluOpType.max

P = 128
PACK = 4
QUADS = 4
QUAD = P // QUADS
ROWS = 4
LIST = 16
MX_ALIGN = 64
M_TILES = N // P
HALF_J = J // 2
HALF_O = O // 2
LINE = 4


def tile_list_gatedladder_solo_one_pairweighed_kernel(
    tc, xt_words, xt_scales, w_words, w_scales, sa, sb, sg, bg, wb_words, wb_scales, so, sp,
    offs, offs2, offs3, offs4, offs5, offs6, offs7, out,
):
    nc = tc.nc

    def entries(lst, first, count):
        return lst[:, first // LIST : (first + count) // LIST]

    with ExitStack() as ctx:
        keep = ctx.enter_context(tc.tile_pool(name="keep", bufs=1))
        psum = ctx.enter_context(tc.psum_pool(name="psum", bufs=1))

        def load_list(src, name):
            lst = keep.tile([P, src.shape[1]], U16, name=name)
            nc.sync.dma_start(lst[:], src)
            return lst

        def load_scale_plane(plane, scales):
            for q in range(QUADS):
                nc.sync.dma_start(
                    out=plane[QUAD * q : QUAD * q + ROWS, :].bitcast(I32),
                    in_=scales[0, ROWS * q : ROWS * (q + 1), :].bitcast(I32),
                )

        def load_by_slice(src, name):
            vec = keep.tile([P, PACK], F32, name=name)
            nc.sync.dma_start(out=vec[:], in_=src.rearrange("(p t) one -> p (t one)", t=PACK))
            return vec

        def zeroed_board(t, **place):
            board = keep.tile([P, 2 * C], F32, name="pw%d" % t, **place)
            nc.vector.memset(board[:, :C].bitcast(I32), 0)
            return board

        xs = keep.tile([P, T], U8, name="xs", tag="xs", align_bytes=MX_ALIGN)
        nc.vector.memset(xs[:].bitcast(I32), 0)
        warm = keep.tile([P, 2], F32, name="warm")
        nc.vector.memset(warm[:, 0:1], 0.0)
        ws = keep.tile([P, R], U8, name="ws")
        nc.vector.memset(ws[:].bitcast(I32), 0)
        pw = [zeroed_board(t) for t in range(PACK - 1)]
        wbs = keep.tile([P, N], U8, name="wbs", align_bytes=MX_ALIGN)
        nc.vector.memset(wbs[:].bitcast(I32), 0)

        ws_rows = keep.tile([ROWS, QUADS, R // 4], I32, name="ws_rows")
        nc.sync.dma_start(out=ws_rows[:], in_=w_scales[0].bitcast(I32).rearrange("(q r) c -> r q c", r=ROWS))
        xw = keep.tile([P, T], U16, name="xw")
        nc.sync.dma_start(out=xw[:].bitcast(I32), in_=xt_words[0].bitcast(I32))
        l1 = load_list(offs, "l1")
        ww = keep.tile([P, R], U32, name="ww")
        nc.scalar.dma_start(out=ww[:].bitcast(I32), in_=w_words[0].rearrange("p c b -> p (c b)").bitcast(I32))
        load_scale_plane(xs, xt_scales)
        nc.scalar.activation(out=warm[:, 1:2], in_=warm[:, 0:1], func=SIGMOID)
        l2 = load_list(offs2, "l2")
        l4 = load_list(offs4, "l4")
        l3 = load_list(offs3, "l3")
        sg_t = load_by_slice(sg, "sg_t")
        sa_t = load_by_slice(sa, "sa_t")
        bg_t = load_by_slice(bg, "bg_t")
        l5 = load_list(offs5, "l5")
        sb_t = load_by_slice(sb, "sb_t")
        wbw = keep.tile([P, 2 * N], U8, name="wbw", align_bytes=MX_ALIGN)
        nc.sync.dma_start(out=wbw[:].bitcast(I32), in_=wb_words[0].bitcast(I32))
        load_scale_plane(wbs, wb_scales)
        l6 = load_list(offs6, "l6")
        l7 = load_list(offs7, "l7")
        so_t = keep.tile([P, M_TILES], F32, name="so_t")
        sp_t = keep.tile([P, M_TILES], F32, name="sp_t")
        with nc.allow_non_contiguous_dma(reason="one float32 weight for each partition and output tile"):
            nc.sync.dma_start(out=so_t[:], in_=so.rearrange("(m p) one -> p (m one)", p=P))
            nc.sync.dma_start(out=sp_t[:], in_=sp.rearrange("(m p) one -> p (m one)", p=P))

        for q in range(QUADS):
            nc.vector.tensor_copy(out=ws[QUAD * q : QUAD * q + ROWS, :].bitcast(I32), in_=ws_rows[:, q, :])
        ws_by_slice = ws[:].rearrange("p (m t) -> p t m", t=PACK)
        ww_by_column = ww[:].rearrange("p (m t) -> p m t", t=PACK)
        wsd0 = keep.tile([P, P], U8, name="wsd0", align_bytes=MX_ALIGN)
        wwd0 = keep.tile([P, P], U32, name="wwd0", tag="wwd0", align_bytes=MX_ALIGN)
        wwd = keep.tile([P, PACK - 1, P], U32, name="wwd", align_bytes=MX_ALIGN)
        nc.scalar.copy(out=wwd0[:], in_=ww_by_column[:, :, 0])
        nc.scalar.copy(out=wwd[:].rearrange("p t m -> p m t"), in_=ww_by_column[:, :, 1:])

        xsg = keep.tile([P, J], U8, name="xsg", align_bytes=MX_ALIGN)
        xwg = keep.tile([P, J], U16, name="xwg", align_bytes=MX_ALIGN)
        a_sb = keep.tile([P, PACK, J], F32, name="a_sb", tag="a_then_prod")

        def first_matmul(acc, words, scale_bytes, slots):
            nc.tensor.matmul_mx(
                out=acc, lhsT=words.bitcast(E4M3X4), lhsT_scale=scale_bytes,
                rhs=xwg[:, slots].bitcast(E2M1X4), rhs_scale=xsg[:, slots], start=True, stop=True,
            )

        def slice0_half(h):
            slots = slice(h * HALF_J, (h + 1) * HALF_J)
            nc.vector.tensor_copy(out=xsg[:, slots], in_=xs[:].indirect(entries(l1, h * HALF_J, HALF_J)))
            acc = psum.tile([P, HALF_J], F32, name="a0_%d" % h)
            first_matmul(acc[:], wwd0[:], wsd0[:], slots)
            return acc

        def slice0_put(h):
            nc.scalar.activation(
                out=pw[0][:].indirect(entries(l2, h * HALF_J, HALF_J)),
                in_=a_sb[:, 0, h * HALF_J : (h + 1) * HALF_J], func=COPY,
            )

        nc.vector.tensor_copy(out=xwg[:], in_=xw[:].indirect(l1[:]))
        nc.vector.tensor_copy(out=wsd0[:], in_=ws_by_slice[:, 0, :])
        acc = slice0_half(0)
        nc.scalar.copy(out=a_sb[:, 0, :HALF_J], in_=acc[:])
        slice0_put(0)
        acc = slice0_half(1)
        wsd = keep.tile([P, PACK - 1, P], U8, name="wsd", tag="xs", align_bytes=MX_ALIGN)
        nc.vector.tensor_copy(out=wsd[:], in_=ws_by_slice[:, 1:, :])
        nc.vector.tensor_copy(out=a_sb[:, 0, HALF_J:], in_=acc[:])
        slice0_put(1)
        pw.append(zeroed_board(PACK - 1, tag="wwd0", align_bytes=MX_ALIGN))

        for first, count in ((1, 2), (3, 1)):
            acc = psum.tile([P, count, J], F32, name="a%d" % first)
            for i in range(count):
                first_matmul(acc[:, i, :], wwd[:, first + i - 1, :], wsd[:, first + i - 1, :], slice(0, J))
            nc.vector.tensor_copy(out=a_sb[:, first : first + count, :], in_=acc[:])
        for t in range(1, PACK):
            nc.vector.tensor_copy(out=pw[t][:].indirect(l2[:]), in_=a_sb[:, t, :])

        pg = [keep.tile([P, C], F32, name="pg%d" % t) for t in range(PACK)]
        gate = keep.tile([P, PACK * C], F32, name="gate")
        val = keep.tile([P, PACK * C], F32, name="val")
        prod = keep.tile([P, PACK * C], F32, name="prod", tag="a_then_prod")

        def fetch_gate(t):
            nc.scalar.activation(
                out=gate[:, t * C : (t + 1) * C], in_=pw[t][:].indirect(l4[:]), func=SIGMOID,
                bias=bg_t[:, t : t + 1], scale=sg_t[:, t : t + 1],
            )

        def fetch_val(t, c0, width):
            nc.scalar.activation(
                out=val[:, t * C + c0 : t * C + c0 + width], in_=pw[t][:].indirect(entries(l3, c0, width)),
                func=COPY, scale=sa_t[:, t : t + 1],
            )

        def multiply(start, width):
            run = slice(start, start + width)
            nc.vector.tensor_tensor(out=prod[:, run], in0=val[:, run], in1=gate[:, run], op=MULT)

        def keep_larger(t, c0, width):
            nc.vector.tensor_tensor(
                out=pg[t][:, c0 : c0 + width], in0=pw[t][:, c0 : c0 + width],
                in1=prod[:, t * C + c0 : t * C + c0 + width], op=MAX,
            )

        for t in range(2):
            fetch_gate(t)
            fetch_val(t, 0, C)
        multiply(0, 2 * C)
        for t in range(2):
            keep_larger(t, 0, C)
        for t, width in ((2, C), (3, C // 2)):
            fetch_gate(t)
            for c0 in range(0, C, width):
                fetch_val(t, c0, width)
                multiply(t * C + c0, width)
                keep_larger(t, c0, width)

        p_sb = [keep.tile([P, O], F32, name="p_sb%d" % m) for m in range(M_TILES)]
        hid = [keep.tile([P, PACK, HALF_O], F32, name="hid%d" % h) for h in range(2)]

        def pick(h, t):
            nc.scalar.activation(
                out=hid[h][:, t, :], in_=pg[t][:].indirect(entries(l5, h * HALF_O, HALF_O)),
                func=COPY, scale=sb_t[:, t : t + 1],
            )

        def second_stage(h):
            woven = keep.tile([P, HALF_O, PACK], BF16, name="woven%d" % h, align_bytes=MX_ALIGN)
            nc.vector.tensor_copy(
                out=woven[:].rearrange("p (c i) t -> p c t i", i=LINE),
                in_=hid[h][:].rearrange("p t (c i) -> p c t i", i=LINE),
            )
            codes = keep.tile([P, HALF_O], U32, name="codes%d" % h, align_bytes=MX_ALIGN)
            plane = keep.tile([P, HALF_O], U8, name="hs%d" % h, align_bytes=MX_ALIGN)
            nc.vector.quantize_mx(
                out=codes[:].bitcast(E5M2X4), scales=plane[:], in_=woven[:].rearrange("p o t -> p (o t)"),
            )
            sums = []
            for m in range(M_TILES):
                bank = psum.tile([P, HALF_O], F32, name=("a0_%d", "p1_%d")[h] % m)
                nc.tensor.matmul_mx(
                    out=bank[:], lhsT=wbw[:, 2 * P * m : 2 * P * (m + 1)].bitcast(E2M1X4),
                    lhsT_scale=wbs[:, P * m : P * (m + 1)],
                    rhs=codes[:].bitcast(E5M2X4), rhs_scale=plane[:], start=True, stop=True,
                )
                sums.append(bank)
            return sums

        for t in range(PACK - 1):
            pick(0, t)
        pick(1, 0)
        pick(0, PACK - 1)
        first_half = second_stage(0)
        for t in range(1, PACK):
            pick(1, t)
        second_half = second_stage(1)
        for m in range(M_TILES):
            nc.scalar.copy(out=p_sb[m][:, :HALF_O], in_=first_half[m][:])
        nc.scalar.copy(out=p_sb[0][:, HALF_O:], in_=second_half[0][:])
        nc.vector.tensor_copy(out=p_sb[1][:, HALF_O:], in_=second_half[1][:])

        for m in range(M_TILES):
            left = keep.tile([P, U], F32, name="left%d" % m)
            right = keep.tile([P, U], F32, name="right%d" % m)
            y = keep.tile([P, U], F32, name="y%d" % m)
            nc.scalar.activation(out=left[:], in_=p_sb[m][:].indirect(l6[:]), func=COPY, scale=so_t[:, m : m + 1])
            nc.scalar.activation(out=right[:], in_=p_sb[m][:].indirect(l7[:]), func=COPY, scale=sp_t[:, m : m + 1])
            nc.vector.tensor_tensor(out=y[:], in0=left[:], in1=right[:], op=MAX)
            nc.sync.dma_start(out=out[P * m : P * (m + 1), :], in_=y[:])
